import numpy as np
import ml_dtypes


def mxq(x, axis, fmt="e4m3"):
    dtype, down = {"e4m3": (ml_dtypes.float8_e4m3fn, 7), "e5m2": (ml_dtypes.float8_e5m2, 14)}[fmt]
    v = np.moveaxis(np.asarray(x, np.float32).astype(ml_dtypes.bfloat16).astype(np.float64), axis, -1)
    blocks = v.reshape(v.shape[:-1] + (-1, 32))
    amax = np.abs(blocks).max(-1, keepdims=True)
    byte = np.maximum(np.where(amax > 0, np.frexp(amax)[1] - 1 + 127, 0) - down, 1)
    scale = np.exp2(byte - 127.0)
    codes = (blocks / scale).astype(np.float32).astype(dtype).astype(np.float64)
    return np.moveaxis((codes * scale).reshape(v.shape), -1, axis)


WIDE = False


def mx_kscale(k):
    if not WIDE:
        return np.ones(k)
    levels = np.array([10, -10, 5, -5, 0])
    if k % 512:
        return np.exp2(np.random.permutation(np.resize(levels, k // 32))).repeat(32)
    a = np.empty((k // 512, 16))
    for p in range(k // 512):
        a[p, :8] = np.random.permutation(np.resize(levels, 8))
        for g in range(8):
            far = levels[np.abs(levels - a[p, g]) >= 10]
            a[p, g + 8] = far[np.random.randint(len(far))]
    return np.exp2(a.ravel()).repeat(32)


def f64(x):
    return np.asarray(x).astype(np.float64)


def striped(idx):
    return np.tile(idx.reshape(-1, 16).T, (8, 1)).astype(np.uint16)


def unstriped(offs):
    return offs[:16].T.reshape(-1).astype(np.int64)


def striped8(idx):
    return np.concatenate([x.reshape(-1, 16).T for x in idx]).astype(np.uint16)


def runs(offs, k):
    lists = np.stack([offs[16 * r : 16 * r + 16].T.reshape(-1) for r in range(8)]).astype(np.int64)
    return lists[np.arange(k) % 512 // 64]


def pack_weight(w):
    k, n = w.shape
    w = f64(np.asarray(w, np.float32).astype(ml_dtypes.bfloat16)).reshape(k // 32, 32, n)
    amax = np.abs(w).max(1)
    byte = np.clip(np.where(amax > 0, np.frexp(amax)[1] - 1 + 127 - 7, 1), 1, 254)
    scaled = (w * np.exp2(127.0 - byte)[:, None, :]).reshape(k, n).astype(np.float32)
    words = np.ascontiguousarray(scaled.reshape(k // 512, 128, 4, n).transpose(0, 1, 3, 2)).astype(ml_dtypes.float8_e4m3fn).view(np.uint8)
    return words, np.ascontiguousarray(byte.astype(np.uint8).reshape(k // 512, 16, n))


def unpack_weight(words, scales):
    g, p, n, _ = words.shape
    vals = np.ascontiguousarray(words).view(ml_dtypes.float8_e4m3fn).astype(np.float64) * np.repeat(np.exp2(scales.astype(np.float64) - 127.0), 8, axis=1)[..., None]
    return vals.transpose(0, 1, 3, 2).reshape(g * 512, n)


def sigmoid(v):
    return 1.0 / (1.0 + np.exp(-np.maximum(v, -700.0)))


K, T, S, G, H, W = 512, 2048, 512, 2048, 512, 256


def setup_inputs():
    n = np.random.standard_normal
    s = mx_kscale(K)[:, None]
    u = mx_kscale(S)
    packed_xT = pack_weight(n((K, T)) * s)
    packed_dT = pack_weight(n((K, G)) / s)
    perm = np.stack([np.random.permutation(S) for _ in range(8)])
    return {
        "x_words": packed_xT[0],
        "x_scales": packed_xT[1],
        "d_words": packed_dT[0],
        "d_scales": packed_dT[1],
        "ga": (np.random.uniform(0.5, 1.5, (H, 1)) * u[:, None]).astype(np.float32),
        "gb": (np.random.uniform(0.5, 1.5, (H, 1)) / u[:, None]).astype(np.float32),
        "offs": striped(np.random.permutation(T)[:S]),
        "kidx": striped8(np.random.randint(0, G, (8, H))),
        "n1": striped8(np.stack([np.random.permutation(S) for _ in range(8)])),
        "n2": striped8(np.stack([np.random.permutation(S) for _ in range(8)])),
        "n3": striped8(np.stack([np.random.permutation(S) for _ in range(8)])),
        "n4": striped8(np.stack([np.random.permutation(S) for _ in range(8)])),
        "n5": striped8(perm[:, :W]),
        "n6": striped8(perm[:, W:]),
    }


def reference(x_words, x_scales, d_words, d_scales, ga, gb, offs, kidx, n1, n2, n3, n4, n5, n6):
    d_kidx = unpack_weight(d_words, d_scales)[np.arange(K)[:, None], runs(kidx, K)]
    xq = unpack_weight(x_words, x_scales)[:, unstriped(offs)]
    s = 0.0625 * (d_kidx.T @ xq)
    st = s * (sigmoid(s[np.arange(H)[:, None], runs(n1, H)]))
    z = f64(ga) * (st - (st[np.arange(H)[:, None], runs(n2, H)]))
    z2 = f64(gb) * ((s - (s[np.arange(H)[:, None], runs(n3, H)])) * (sigmoid(s[np.arange(H)[:, None], runs(n4, H)])))
    cm = 0.0625 * ((mxq(z, 0, "e4m3").T @ mxq(z2, 0, "e4m3")))
    pa = cm[np.arange(S)[:, None], runs(n5, S)]
    pb = cm[np.arange(S)[:, None], runs(n6, S)]
    rb = np.minimum(pa, pb)
    ra = np.maximum(pa, pb)
    ds = np.zeros((S, S))
    ds[np.arange(S)[:, None], runs(n5, S)] = ra
    out = ds.copy()
    out[np.arange(S)[:, None], runs(n6, S)] = rb
    return out

@@ -1,0 +1,221 @@
+from contextlib import ExitStack
+
+import concourse.mybir as mybir
+
+K, T, S, G, H, W = 512, 2048, 512, 2048, 512, 256
+FLOPS = 2 * K * H * S + 2 * H * S * S
+
+F32 = mybir.dt.float32
+BF16 = mybir.dt.bfloat16
+I32 = mybir.dt.int32
+U32 = mybir.dt.uint32
+U16 = mybir.dt.uint16
+U8 = mybir.dt.uint8
+FP8X4 = mybir.dt.float8_e4m3fn_x4
+ALU = mybir.AluOpType
+ACT = mybir.ActivationFunctionType
+
+P = 128
+PACK = 4
+HALF = S // 2
+SIXTEENTH = 0.0625
+
+
+def tile_picked_simkhopggdiforder_none_p_kernel(
+    tc, x_words, x_scales, d_words, d_scales, ga, gb, offs, kidx, n1, n2, n3, n4, n5, n6, out
+):
+    nc = tc.nc
+    with ExitStack() as ctx:
+        keep = ctx.enter_context(tc.tile_pool(name="keep", bufs=1))
+        ring = ctx.enter_context(tc.tile_pool(name="ring", bufs=2))
+        psum = ctx.enter_context(tc.psum_pool(name="psum", bufs=1))
+
+        def load_list(name, src):
+            tile = keep.tile(list(src.shape), U16, name=name)
+            nc.sync.dma_start(tile[:], src)
+            return tile
+
+        def half_of(lst, h):
+            return lst[:, h * (HALF // 16) : (h + 1) * (HALF // 16)]
+
+        d_word_tab = keep.tile([P, G], U32, name="d_word_tab")
+        x_word_tab = keep.tile([P, T], U32, name="x_word_tab")
+        d_byte_tab = keep.tile([P, G], U8, name="d_byte_tab")
+        x_byte_tab = keep.tile([P, T], U8, name="x_byte_tab")
+        nc.scalar.dma_start(d_word_tab[:].bitcast(I32), d_words[0].rearrange("p n t -> p (n t)").bitcast(I32))
+        nc.scalar.dma_start(x_word_tab[:].bitcast(I32), x_words[0].rearrange("p n t -> p (n t)").bitcast(I32))
+
+        kidx_sb = load_list("kidx_sb", kidx)
+        d_rows = d_scales[0].bitcast(I32).rearrange("(r i) c -> i r c", i=2)
+        for i in range(2):
+            nc.sync.dma_start(
+                d_byte_tab[:].bitcast(I32)[i:P:2, :], d_rows[i].unsqueeze(1).broadcast_to([8, 8, G // 4])
+            )
+        offs_sb = load_list("offs_sb", offs)
+        n1_sb = load_list("n1_sb", n1)
+        n3_sb = load_list("n3_sb", n3)
+        n4_sb = load_list("n4_sb", n4)
+        n2_sb = load_list("n2_sb", n2)
+        n5_sb = load_list("n5_sb", n5)
+        n6_sb = load_list("n6_sb", n6)
+
+        x_rows = x_scales[0].bitcast(I32)
+        for q in range(4):
+            nc.gpsimd.dma_start(
+                x_byte_tab[:].bitcast(I32)[32 * q : 32 * q + 32, :],
+                x_rows[4 * q : 4 * q + 4, :].unsqueeze(0).broadcast_to([8, 4, T // 4]),
+            )
+        ga_sb = keep.tile([P, PACK], F32, name="ga_sb")
+        gb_sb = keep.tile([P, PACK], F32, name="gb_sb")
+        nc.gpsimd.dma_start(ga_sb[:], ga.rearrange("(p t) o -> p (t o)", t=PACK))
+        nc.gpsimd.dma_start(gb_sb[:], gb.rearrange("(p t) o -> p (t o)", t=PACK))
+
+        key_bytes = keep.tile([P, H], U8, name="key_bytes")
+        nc.vector.tensor_copy(key_bytes[:], d_byte_tab[:].indirect(kidx_sb[:]))
+        key_bytes_dealt = keep.tile([P, H], U8, name="key_bytes_dealt")
+        nc.vector.tensor_copy(
+            key_bytes_dealt[:].rearrange("p (t m) -> p t m", t=PACK),
+            key_bytes[:].rearrange("p (m t) -> p t m", t=PACK),
+        )
+        key_scales = keep.tile([P, H], U8, name="key_scales", align_bytes=64)
+        nc.vector.tensor_copy(key_scales[:].bitcast(I32), key_bytes_dealt[:].bitcast(I32))
+        for i in range(2):
+            nc.scalar.dma_start(
+                key_scales[:].bitcast(I32)[2 + i : P : 32, :], key_bytes_dealt[:].bitcast(I32)[16 + i : P : 32, :]
+            )
+
+        key_words = keep.tile([P, H], U32, name="key_words")
+        nc.vector.tensor_copy(key_words[:], d_word_tab[:].indirect(kidx_sb[:]))
+        key_codes = keep.tile([P, H], U32, name="key_codes", align_bytes=64)
+        nc.vector.tensor_copy(
+            key_codes[:].rearrange("p (t m) -> p m t", t=PACK),
+            key_words[:].rearrange("p (m t) -> p m t", t=PACK),
+        )
+        tok_scales = keep.tile([P, S], U8, name="tok_scales", align_bytes=64)
+        nc.vector.tensor_copy(tok_scales[:], x_byte_tab[:].indirect(offs_sb[:]))
+        tok_codes = keep.tile([P, S], U32, name="tok_codes", align_bytes=64)
+        nc.vector.tensor_copy(tok_codes[:], x_word_tab[:].indirect(offs_sb[:]))
+
+        s_sb = [keep.tile([P, S], F32, name="s%d" % t) for t in range(PACK)]
+        st_sb = [keep.tile([P, S], F32, name="st%d" % t) for t in range(PACK)]
+        sig_at_n1 = keep.tile([P, PACK, S], F32, name="sig_at_n1")
+        s_at_n3 = keep.tile([P, PACK, S], F32, name="s_at_n3")
+        st_all = keep.tile([P, PACK, S], F32, name="st_all")
+        st_at_n2 = keep.tile([P, PACK, S], F32, name="st_at_n2")
+        diff = keep.tile([P, PACK, S], F32, name="diff")
+        sig_at_n4 = keep.tile([P, PACK, S], F32, name="sig_at_n4")
+
+        def hcols(h):
+            return slice(h * HALF, (h + 1) * HALF)
+
+        def scores(t):
+            cols = slice(t * P, (t + 1) * P)
+            s_ps = psum.tile([P, S], F32, name="s_bank")
+            nc.tensor.matmul_mx(
+                out=s_ps[:],
+                lhsT=key_codes[:, cols].bitcast(FP8X4),
+                lhsT_scale=key_scales[:, cols],
+                rhs=tok_codes[:].bitcast(FP8X4),
+                rhs_scale=tok_scales[:],
+                start=True,
+                stop=True,
+            )
+            if t == 0:
+                nc.vector.tensor_scalar(s_sb[t][:], s_ps[:], SIXTEENTH, None, ALU.mult)
+            else:
+                nc.scalar.activation(s_sb[t][:], s_ps[:], ACT.Copy, scale=SIXTEENTH)
+            for h in range(2):
+                nc.scalar.activation(sig_at_n1[:, t, hcols(h)], s_sb[t][:].indirect(half_of(n1_sb, h)), ACT.Sigmoid)
+
+        def fetch_n3(t, h):
+            nc.vector.tensor_copy(s_at_n3[:, t, hcols(h)], s_sb[t][:].indirect(half_of(n3_sb, h)))
+
+        def weigh_diff(t):
+            nc.vector.tensor_scalar(diff[:, t, :], diff[:, t, :], gb_sb[:, t : t + 1], None, ALU.mult)
+
+        def fetch_n2(t, h, on_vector):
+            window = st_sb[t][:].indirect(half_of(n2_sb, h))
+            if on_vector:
+                nc.vector.tensor_copy(st_at_n2[:, t, hcols(h)], window)
+            else:
+                nc.scalar.activation(st_at_n2[:, t, hcols(h)], window, ACT.Copy)
+
+        for t in range(PACK):
+            scores(t)
+            fetch_n3(t, 0)
+            if t > 0:
+                weigh_diff(t - 1)
+            fetch_n3(t, 1)
+            nc.vector.scalar_tensor_tensor(
+                st_sb[t][:], s_sb[t][:], ga_sb[:, t : t + 1], sig_at_n1[:, t, :], ALU.mult, ALU.mult
+            )
+            nc.sync.dma_start(st_all[:, t, :], st_sb[t][:])
+            nc.vector.tensor_tensor(diff[:, t, :], s_sb[t][:], s_at_n3[:, t, :], ALU.subtract)
+
+        for h in range(2):
+            for t in range(PACK):
+                nc.scalar.activation(sig_at_n4[:, t, hcols(h)], s_sb[t][:].indirect(half_of(n4_sb, h)), ACT.Sigmoid)
+
+        z2_codes = keep.tile([P, S], U32, name="z2_codes", align_bytes=64)
+        z2_scales = keep.tile([P, S], U8, name="z2_scales", align_bytes=64)
+        z2_bf = [keep.tile([P, PACK * HALF], BF16, name="z2_bf%d" % h, align_bytes=64) for h in range(2)]
+
+        def make_z2(h):
+            nc.vector.tensor_tensor(
+                z2_bf[h][:].rearrange("p (c i t) -> p c t i", i=2, t=PACK),
+                diff[:, :, hcols(h)].rearrange("p t (c i) -> p c t i", i=2),
+                sig_at_n4[:, :, hcols(h)].rearrange("p t (c i) -> p c t i", i=2),
+                ALU.mult,
+            )
+
+        def quantise_z2(h):
+            nc.vector.quantize_mx(out=z2_codes[:, hcols(h)].bitcast(FP8X4), scales=z2_scales[:, hcols(h)], in_=z2_bf[h][:])
+
+        fetch_n2(0, 0, True)
+        weigh_diff(PACK - 1)
+        fetch_n2(0, 1, True)
+        make_z2(0)
+        fetch_n2(1, 0, True)
+        quantise_z2(0)
+        make_z2(1)
+        for t, h in [(1, 1), (2, 0), (2, 1), (3, 0), (3, 1)]:
+            fetch_n2(t, h, False)
+        quantise_z2(1)
+
+        z_bf = [keep.tile([P, PACK * P], BF16, name="z_bf%d" % u, align_bytes=64) for u in range(PACK)]
+        z_codes = [keep.tile([P, P], U32, name="z_codes%d" % u, align_bytes=64) for u in range(PACK)]
+        z_scales = [keep.tile([P, P], U8, name="z_scales%d" % u, align_bytes=64) for u in range(PACK)]
+        st_pairs = st_all[:].rearrange("p t (c u i) -> p u c t i", u=PACK, i=2)
+        n2_pairs = st_at_n2[:].rearrange("p t (c u i) -> p u c t i", u=PACK, i=2)
+        for u in range(PACK):
+            nc.vector.tensor_tensor(
+                z_bf[u][:].rearrange("p (c i t) -> p c t i", i=2, t=PACK), st_pairs[:, u], n2_pairs[:, u], ALU.subtract
+            )
+            nc.vector.quantize_mx(out=z_codes[u][:].bitcast(FP8X4), scales=z_scales[u][:], in_=z_bf[u][:])
+
+        out_rows = out.rearrange("(c u i) n -> u c i n", u=PACK, i=2)
+        for u in range(PACK):
+            cm_ps = psum.tile([P, S], F32, name="cm_bank%d" % u)
+            nc.tensor.matmul_mx(
+                out=cm_ps[:],
+                lhsT=z_codes[u][:].bitcast(FP8X4),
+                lhsT_scale=z_scales[u][:],
+                rhs=z2_codes[:].bitcast(FP8X4),
+                rhs_scale=z2_scales[:],
+                start=True,
+                stop=True,
+            )
+            cm = keep.tile([P, S], F32, name="cm%d" % u)
+            nc.scalar.activation(cm[:], cm_ps[:], ACT.Copy, scale=SIXTEENTH)
+            pa = keep.tile([P, W], F32, name="pa%d" % u)
+            pb = keep.tile([P, W], F32, name="pb%d" % u)
+            nc.scalar.activation(pa[:], cm[:].indirect(n5_sb[:]), ACT.Copy)
+            nc.scalar.activation(pb[:], cm[:].indirect(n6_sb[:]), ACT.Copy)
+            ra = ring.tile([P, W], F32, name="ra")
+            rb = ring.tile([P, W], F32, name="rb")
+            nc.vector.tensor_tensor(ra[:], pa[:], pb[:], ALU.max)
+            nc.vector.tensor_tensor(rb[:], pa[:], pb[:], ALU.min)
+            placed = keep.tile([P, S], F32, name="placed%d" % u)
+            nc.vector.tensor_copy(placed[:].indirect(n5_sb[:]), ra[:])
+            nc.vector.tensor_copy(placed[:].indirect(n6_sb[:]), rb[:])
+            nc.sync.dma_start(out_rows[u], placed[:])

@@ -38,33 +38,36 @@ def tile_picked_simkhopggdiforder_none_p_kernel(
         def half_of(lst, h):
             return lst[:, h * (HALF // 16) : (h + 1) * (HALF // 16)]
 
+        def hcols(h):
+            return slice(h * HALF, (h + 1) * HALF)
+
         d_word_tab = keep.tile([P, G], U32, name="d_word_tab")
         x_word_tab = keep.tile([P, T], U32, name="x_word_tab")
         d_byte_tab = keep.tile([P, G], U8, name="d_byte_tab")
         x_byte_tab = keep.tile([P, T], U8, name="x_byte_tab")
-        nc.scalar.dma_start(d_word_tab[:].bitcast(I32), d_words[0].rearrange("p n t -> p (n t)").bitcast(I32))
-        nc.scalar.dma_start(x_word_tab[:].bitcast(I32), x_words[0].rearrange("p n t -> p (n t)").bitcast(I32))
 
+        def load_scale_rows(tab, scales):
+            rows = scales[0].bitcast(I32)
+            nc.sync.dma_start(tab[:].bitcast(I32), rows.unsqueeze(1).broadcast_to([16, 8, rows.shape[1]]))
+
+        load_scale_rows(d_byte_tab, d_scales)
         kidx_sb = load_list("kidx_sb", kidx)
-        d_rows = d_scales[0].bitcast(I32).rearrange("(r i) c -> i r c", i=2)
-        for i in range(2):
-            nc.sync.dma_start(
-                d_byte_tab[:].bitcast(I32)[i:P:2, :], d_rows[i].unsqueeze(1).broadcast_to([8, 8, G // 4])
-            )
         offs_sb = load_list("offs_sb", offs)
+        load_scale_rows(x_byte_tab, x_scales)
         n1_sb = load_list("n1_sb", n1)
         n3_sb = load_list("n3_sb", n3)
+        nc.sync.dma_start(d_word_tab[:].bitcast(I32), d_words[0].rearrange("p n t -> p (n t)").bitcast(I32))
+        nc.sync.dma_start(x_word_tab[:].bitcast(I32), x_words[0].rearrange("p n t -> p (n t)").bitcast(I32))
         n4_sb = load_list("n4_sb", n4)
         n2_sb = load_list("n2_sb", n2)
         n5_sb = load_list("n5_sb", n5)
         n6_sb = load_list("n6_sb", n6)
 
-        x_rows = x_scales[0].bitcast(I32)
-        for q in range(4):
-            nc.gpsimd.dma_start(
-                x_byte_tab[:].bitcast(I32)[32 * q : 32 * q + 32, :],
-                x_rows[4 * q : 4 * q + 4, :].unsqueeze(0).broadcast_to([8, 4, T // 4]),
-            )
+        s_win = [keep.tile([P, 2 * S], F32, name="s%d" % t) for t in range(PACK)]
+        st_win = [keep.tile([P, 2 * S], F32, name="st%d" % t) for t in range(PACK)]
+        for t in range(PACK):
+            nc.vector.memset(s_win[t][:, S:], 0.0)
+            nc.gpsimd.memset(st_win[t][:, S:], 0.0)
         ga_sb = keep.tile([P, PACK], F32, name="ga_sb")
         gb_sb = keep.tile([P, PACK], F32, name="gb_sb")
         nc.gpsimd.dma_start(ga_sb[:], ga.rearrange("(p t) o -> p (t o)", t=PACK))
@@ -72,17 +75,19 @@ def tile_picked_simkhopggdiforder_none_p_kernel(
 
         key_bytes = keep.tile([P, H], U8, name="key_bytes")
         nc.vector.tensor_copy(key_bytes[:], d_byte_tab[:].indirect(kidx_sb[:]))
-        key_bytes_dealt = keep.tile([P, H], U8, name="key_bytes_dealt")
+        planes = keep.tile([P, H + S], U8, name="planes", align_bytes=64)
+        plane_words = planes[:].bitcast(I32)
         nc.vector.tensor_copy(
-            key_bytes_dealt[:].rearrange("p (t m) -> p t m", t=PACK),
+            planes[:, :H].rearrange("p (t m) -> p t m", t=PACK),
             key_bytes[:].rearrange("p (m t) -> p t m", t=PACK),
         )
-        key_scales = keep.tile([P, H], U8, name="key_scales", align_bytes=64)
-        nc.vector.tensor_copy(key_scales[:].bitcast(I32), key_bytes_dealt[:].bitcast(I32))
-        for i in range(2):
-            nc.scalar.dma_start(
-                key_scales[:].bitcast(I32)[2 + i : P : 32, :], key_bytes_dealt[:].bitcast(I32)[16 + i : P : 32, :]
-            )
+        tok_bytes = keep.tile([P, S], U8, name="tok_bytes")
+        nc.vector.tensor_copy(tok_bytes[:], x_byte_tab[:].indirect(offs_sb[:]))
+        nc.vector.tensor_copy(plane_words[:, H // 4 :], tok_bytes[:].bitcast(I32))
+        for a in range(1, 4):
+            nc.scalar.dma_start(plane_words[a:P:32, :], plane_words[8 * a : P : 32, :])
+        key_scales = planes[:, :H]
+        tok_scales = planes[:, H:]
 
         key_words = keep.tile([P, H], U32, name="key_words")
         nc.vector.tensor_copy(key_words[:], d_word_tab[:].indirect(kidx_sb[:]))
@@ -91,71 +96,62 @@ def tile_picked_simkhopggdiforder_none_p_kernel(
             key_codes[:].rearrange("p (t m) -> p m t", t=PACK),
             key_words[:].rearrange("p (m t) -> p m t", t=PACK),
         )
-        tok_scales = keep.tile([P, S], U8, name="tok_scales", align_bytes=64)
-        nc.vector.tensor_copy(tok_scales[:], x_byte_tab[:].indirect(offs_sb[:]))
         tok_codes = keep.tile([P, S], U32, name="tok_codes", align_bytes=64)
-        nc.vector.tensor_copy(tok_codes[:], x_word_tab[:].indirect(offs_sb[:]))
+        for h in range(2):
+            nc.vector.tensor_copy(tok_codes[:, hcols(h)], x_word_tab[:].indirect(half_of(offs_sb, h)))
 
-        s_sb = [keep.tile([P, S], F32, name="s%d" % t) for t in range(PACK)]
-        st_sb = [keep.tile([P, S], F32, name="st%d" % t) for t in range(PACK)]
+        s_sb = [win[:, :S] for win in s_win]
+        st_sb = [win[:, :S] for win in st_win]
         sig_at_n1 = keep.tile([P, PACK, S], F32, name="sig_at_n1")
-        s_at_n3 = keep.tile([P, PACK, S], F32, name="s_at_n3")
+        s_all = keep.tile([P, PACK, S], F32, name="s_all")
         st_all = keep.tile([P, PACK, S], F32, name="st_all")
         st_at_n2 = keep.tile([P, PACK, S], F32, name="st_at_n2")
         diff = keep.tile([P, PACK, S], F32, name="diff")
         sig_at_n4 = keep.tile([P, PACK, S], F32, name="sig_at_n4")
 
-        def hcols(h):
-            return slice(h * HALF, (h + 1) * HALF)
-
-        def scores(t):
+        def scores(t, bank, toks):
             cols = slice(t * P, (t + 1) * P)
-            s_ps = psum.tile([P, S], F32, name="s_bank")
             nc.tensor.matmul_mx(
-                out=s_ps[:],
+                out=bank,
                 lhsT=key_codes[:, cols].bitcast(FP8X4),
                 lhsT_scale=key_scales[:, cols],
-                rhs=tok_codes[:].bitcast(FP8X4),
-                rhs_scale=tok_scales[:],
+                rhs=tok_codes[:, toks].bitcast(FP8X4),
+                rhs_scale=tok_scales[:, toks],
                 start=True,
                 stop=True,
             )
-            if t == 0:
-                nc.vector.tensor_scalar(s_sb[t][:], s_ps[:], SIXTEENTH, None, ALU.mult)
-            else:
-                nc.scalar.activation(s_sb[t][:], s_ps[:], ACT.Copy, scale=SIXTEENTH)
-            for h in range(2):
-                nc.scalar.activation(sig_at_n1[:, t, hcols(h)], s_sb[t][:].indirect(half_of(n1_sb, h)), ACT.Sigmoid)
 
-        def fetch_n3(t, h):
-            nc.vector.tensor_copy(s_at_n3[:, t, hcols(h)], s_sb[t][:].indirect(half_of(n3_sb, h)))
-
-        def weigh_diff(t):
-            nc.vector.tensor_scalar(diff[:, t, :], diff[:, t, :], gb_sb[:, t : t + 1], None, ALU.mult)
-
-        def fetch_n2(t, h, on_vector):
-            window = st_sb[t][:].indirect(half_of(n2_sb, h))
-            if on_vector:
-                nc.vector.tensor_copy(st_at_n2[:, t, hcols(h)], window)
-            else:
-                nc.scalar.activation(st_at_n2[:, t, hcols(h)], window, ACT.Copy)
-
-        for t in range(PACK):
-            scores(t)
-            fetch_n3(t, 0)
-            if t > 0:
-                weigh_diff(t - 1)
-            fetch_n3(t, 1)
-            nc.vector.scalar_tensor_tensor(
-                st_sb[t][:], s_sb[t][:], ga_sb[:, t : t + 1], sig_at_n1[:, t, :], ALU.mult, ALU.mult
-            )
-            nc.sync.dma_start(st_all[:, t, :], st_sb[t][:])
-            nc.vector.tensor_tensor(diff[:, t, :], s_sb[t][:], s_at_n3[:, t, :], ALU.subtract)
+        def sigmoid_at(dst, lst, t):
+            nc.scalar.activation(dst[:, t, :], s_win[t][:].indirect(lst[:]), ACT.Sigmoid)
 
         for h in range(2):
-            for t in range(PACK):
-                nc.scalar.activation(sig_at_n4[:, t, hcols(h)], s_sb[t][:].indirect(half_of(n4_sb, h)), ACT.Sigmoid)
+            bank = psum.tile([P, HALF], F32, name="half_bank%d" % h)
+            scores(0, bank[:], hcols(h))
+            nc.vector.tensor_scalar(s_win[0][:, hcols(h)], bank[:], SIXTEENTH, None, ALU.mult)
+        nc.sync.dma_start(s_all[:, 0, :], s_sb[0])
+        for t in range(1, PACK):
+            bank = psum.tile([P, S], F32, name="s_bank%d" % t)
+            scores(t, bank[:], slice(0, S))
+            nc.vector.tensor_scalar(s_sb[t], bank[:], SIXTEENTH, None, ALU.mult)
+            nc.sync.dma_start(s_all[:, t, :], s_sb[t])
+        for t in range(PACK):
+            sigmoid_at(sig_at_n1, n1_sb, t)
+        for t in range(PACK):
+            sigmoid_at(sig_at_n4, n4_sb, t)
 
+        def weigh_diff(t):
+            nc.vector.tensor_scalar(diff[:, t, :], diff[:, t, :], gb_sb[:, t : t + 1], -1.0, ALU.mult, ALU.mult)
+
+        for t in range(PACK):
+            nc.vector.scalar_tensor_tensor(
+                st_sb[t], s_sb[t], ga_sb[:, t : t + 1], sig_at_n1[:, t, :], ALU.mult, ALU.mult
+            )
+            nc.sync.dma_start(st_all[:, t, :], st_sb[t])
+            if t > 0:
+                weigh_diff(t - 1)
+            nc.vector.tensor_tensor(diff[:, t, :], s_win[t][:].indirect(n3_sb[:]), s_all[:, t, :], ALU.subtract)
+
+        last = PACK - 1
         z2_codes = keep.tile([P, S], U32, name="z2_codes", align_bytes=64)
         z2_scales = keep.tile([P, S], U8, name="z2_scales", align_bytes=64)
         z2_bf = [keep.tile([P, PACK * HALF], BF16, name="z2_bf%d" % h, align_bytes=64) for h in range(2)]
@@ -171,51 +167,84 @@ def tile_picked_simkhopggdiforder_none_p_kernel(
         def quantise_z2(h):
             nc.vector.quantize_mx(out=z2_codes[:, hcols(h)].bitcast(FP8X4), scales=z2_scales[:, hcols(h)], in_=z2_bf[h][:])
 
-        fetch_n2(0, 0, True)
-        weigh_diff(PACK - 1)
-        fetch_n2(0, 1, True)
+        nc.vector.tensor_copy(st_at_n2[:, 0, :], st_win[0][:].indirect(n2_sb[:]))
+        weigh_diff(last)
+        for t in range(1, PACK):
+            nc.scalar.activation(st_at_n2[:, t, :], st_win[t][:].indirect(n2_sb[:]), ACT.Copy)
         make_z2(0)
-        fetch_n2(1, 0, True)
-        quantise_z2(0)
         make_z2(1)
-        for t, h in [(1, 1), (2, 0), (2, 1), (3, 0), (3, 1)]:
-            fetch_n2(t, h, False)
-        quantise_z2(1)
+        quantise_z2(0)
 
         z_bf = [keep.tile([P, PACK * P], BF16, name="z_bf%d" % u, align_bytes=64) for u in range(PACK)]
         z_codes = [keep.tile([P, P], U32, name="z_codes%d" % u, align_bytes=64) for u in range(PACK)]
         z_scales = [keep.tile([P, P], U8, name="z_scales%d" % u, align_bytes=64) for u in range(PACK)]
         st_pairs = st_all[:].rearrange("p t (c u i) -> p u c t i", u=PACK, i=2)
         n2_pairs = st_at_n2[:].rearrange("p t (c u i) -> p u c t i", u=PACK, i=2)
-        for u in range(PACK):
+
+        def make_z(u):
             nc.vector.tensor_tensor(
                 z_bf[u][:].rearrange("p (c i t) -> p c t i", i=2, t=PACK), st_pairs[:, u], n2_pairs[:, u], ALU.subtract
             )
+
+        def quantise_z(u):
             nc.vector.quantize_mx(out=z_codes[u][:].bitcast(FP8X4), scales=z_scales[u][:], in_=z_bf[u][:])
 
+        make_z(0)
+        quantise_z2(1)
+        quantise_z(0)
+        make_z(1)
+        for u in range(2, PACK):
+            make_z(u)
+            quantise_z(u - 1)
+        quantise_z(PACK - 1)
+
         out_rows = out.rearrange("(c u i) n -> u c i n", u=PACK, i=2)
+        pa = keep.tile([P, PACK, W], F32, name="pa")
+        pb = keep.tile([P, PACK, W], F32, name="pb")
+        ra = keep.tile([P, PACK, W], F32, name="ra")
+        rb = keep.tile([P, PACK, W], F32, name="rb")
+        placed = [keep.tile([P, S], F32, name="placed%d" % u) for u in range(PACK)]
         for u in range(PACK):
-            cm_ps = psum.tile([P, S], F32, name="cm_bank%d" % u)
-            nc.tensor.matmul_mx(
-                out=cm_ps[:],
-                lhsT=z_codes[u][:].bitcast(FP8X4),
-                lhsT_scale=z_scales[u][:],
-                rhs=z2_codes[:].bitcast(FP8X4),
-                rhs_scale=z2_scales[:],
-                start=True,
-                stop=True,
-            )
             cm = keep.tile([P, S], F32, name="cm%d" % u)
-            nc.scalar.activation(cm[:], cm_ps[:], ACT.Copy, scale=SIXTEENTH)
-            pa = keep.tile([P, W], F32, name="pa%d" % u)
-            pb = keep.tile([P, W], F32, name="pb%d" % u)
-            nc.scalar.activation(pa[:], cm[:].indirect(n5_sb[:]), ACT.Copy)
-            nc.scalar.activation(pb[:], cm[:].indirect(n6_sb[:]), ACT.Copy)
-            ra = ring.tile([P, W], F32, name="ra")
-            rb = ring.tile([P, W], F32, name="rb")
-            nc.vector.tensor_tensor(ra[:], pa[:], pb[:], ALU.max)
-            nc.vector.tensor_tensor(rb[:], pa[:], pb[:], ALU.min)
-            placed = keep.tile([P, S], F32, name="placed%d" % u)
-            nc.vector.tensor_copy(placed[:].indirect(n5_sb[:]), ra[:])
-            nc.vector.tensor_copy(placed[:].indirect(n6_sb[:]), rb[:])
-            nc.sync.dma_start(out_rows[u], placed[:])
+            pieces = [("first", hcols(0)), ("cm", hcols(1))] if u == 0 else [("cm", slice(0, S))]
+            for tag, cols in pieces:
+                cm_ps = psum.tile([P, cols.stop - cols.start], F32, name="cm_ps", tag=tag)
+                nc.tensor.matmul_mx(
+                    out=cm_ps[:],
+                    lhsT=z_codes[u][:].bitcast(FP8X4),
+                    lhsT_scale=z_scales[u][:],
+                    rhs=z2_codes[:, cols].bitcast(FP8X4),
+                    rhs_scale=z2_scales[:, cols],
+                    start=True,
+                    stop=True,
+                )
+                nc.scalar.activation(cm[:, cols], cm_ps[:], ACT.Copy, scale=SIXTEENTH)
+            nc.scalar.activation(pa[:, u, :], cm[:].indirect(n5_sb[:]), ACT.Copy)
+            nc.scalar.activation(pb[:, u, :], cm[:].indirect(n6_sb[:]), ACT.Copy)
+
+        def larger(a, b):
+            nc.vector.tensor_tensor(ra[:, a:b, :], pa[:, a:b, :], pb[:, a:b, :], ALU.max)
+
+        def smaller(a, b):
+            nc.vector.tensor_tensor(rb[:, a:b, :], pa[:, a:b, :], pb[:, a:b, :], ALU.min)
+
+        def put_larger(u):
+            nc.vector.tensor_copy(placed[u][:].indirect(n5_sb[:]), ra[:, u, :])
+
+        def put_smaller(u):
+            nc.vector.tensor_copy(placed[u][:].indirect(n6_sb[:]), rb[:, u, :])
+            nc.sync.dma_start(out_rows[u], placed[u][:])
+
+        larger(0, 1)
+        put_larger(0)
+        larger(1, 2)
+        smaller(0, 2)
+        put_larger(1)
+        put_smaller(0)
+        put_smaller(1)
+        larger(2, 4)
+        smaller(2, 4)
+        put_larger(2)
+        put_larger(3)
+        put_smaller(2)
+        put_smaller(3)

@@ -17,6 +17,11 @@ ACT = mybir.ActivationFunctionType
 
 P = 128
 PACK = 4
+GROUP = 16
+BLOCK_PARTS = 8
+QUADRANT = 32
+SCALE_ROWS = K // 32
+PAIR = 2
 HALF = S // 2
 SIXTEENTH = 0.0625
 
@@ -27,7 +32,6 @@ def tile_picked_simkhopggdiforder_none_p_kernel(
     nc = tc.nc
     with ExitStack() as ctx:
         keep = ctx.enter_context(tc.tile_pool(name="keep", bufs=1))
-        ring = ctx.enter_context(tc.tile_pool(name="ring", bufs=2))
         psum = ctx.enter_context(tc.psum_pool(name="psum", bufs=1))
 
         def load_list(name, src):
@@ -35,11 +39,11 @@ def tile_picked_simkhopggdiforder_none_p_kernel(
             nc.sync.dma_start(tile[:], src)
             return tile
 
-        def half_of(lst, h):
-            return lst[:, h * (HALF // 16) : (h + 1) * (HALF // 16)]
-
-        def hcols(h):
+        def half_cols(h):
             return slice(h * HALF, (h + 1) * HALF)
+
+        def half_list(lst, h):
+            return lst[:, h * (HALF // GROUP) : (h + 1) * (HALF // GROUP)]
 
         d_word_tab = keep.tile([P, G], U32, name="d_word_tab")
         x_word_tab = keep.tile([P, T], U32, name="x_word_tab")
@@ -48,7 +52,9 @@ def tile_picked_simkhopggdiforder_none_p_kernel(
 
         def load_scale_rows(tab, scales):
             rows = scales[0].bitcast(I32)
-            nc.sync.dma_start(tab[:].bitcast(I32), rows.unsqueeze(1).broadcast_to([16, 8, rows.shape[1]]))
+            nc.sync.dma_start(
+                tab[:].bitcast(I32), rows.unsqueeze(1).broadcast_to([SCALE_ROWS, BLOCK_PARTS, rows.shape[1]])
+            )
 
         load_scale_rows(d_byte_tab, d_scales)
         kidx_sb = load_list("kidx_sb", kidx)
@@ -56,18 +62,17 @@ def tile_picked_simkhopggdiforder_none_p_kernel(
         load_scale_rows(x_byte_tab, x_scales)
         n1_sb = load_list("n1_sb", n1)
         n3_sb = load_list("n3_sb", n3)
-        nc.sync.dma_start(d_word_tab[:].bitcast(I32), d_words[0].rearrange("p n t -> p (n t)").bitcast(I32))
-        nc.sync.dma_start(x_word_tab[:].bitcast(I32), x_words[0].rearrange("p n t -> p (n t)").bitcast(I32))
+        nc.sync.dma_start(d_word_tab[:].bitcast(I32), d_words[0].rearrange("p n r -> p (n r)").bitcast(I32))
+        nc.sync.dma_start(x_word_tab[:].bitcast(I32), x_words[0].rearrange("p n r -> p (n r)").bitcast(I32))
         n4_sb = load_list("n4_sb", n4)
         n2_sb = load_list("n2_sb", n2)
         n5_sb = load_list("n5_sb", n5)
         n6_sb = load_list("n6_sb", n6)
 
-        s_win = [keep.tile([P, 2 * S], F32, name="s%d" % t) for t in range(PACK)]
-        st_win = [keep.tile([P, 2 * S], F32, name="st%d" % t) for t in range(PACK)]
+        s_win = [keep.tile([P, 2 * S], F32, name="s_win%d" % t) for t in range(PACK)]
+        st_win = [keep.tile([P, 2 * S], F32, name="st_win%d" % t) for t in range(PACK)]
         for t in range(PACK):
             nc.vector.memset(s_win[t][:, S:], 0.0)
-            nc.gpsimd.memset(st_win[t][:, S:], 0.0)
         ga_sb = keep.tile([P, PACK], F32, name="ga_sb")
         gb_sb = keep.tile([P, PACK], F32, name="gb_sb")
         nc.gpsimd.dma_start(ga_sb[:], ga.rearrange("(p t) o -> p (t o)", t=PACK))
@@ -75,19 +80,19 @@ def tile_picked_simkhopggdiforder_none_p_kernel(
 
         key_bytes = keep.tile([P, H], U8, name="key_bytes")
         nc.vector.tensor_copy(key_bytes[:], d_byte_tab[:].indirect(kidx_sb[:]))
-        planes = keep.tile([P, H + S], U8, name="planes", align_bytes=64)
-        plane_words = planes[:].bitcast(I32)
+        scale_rows = keep.tile([P, H + S], U8, name="scale_rows", align_bytes=64)
+        scale_rows_i32 = scale_rows[:].bitcast(I32)
         nc.vector.tensor_copy(
-            planes[:, :H].rearrange("p (t m) -> p t m", t=PACK),
+            scale_rows[:, :H].rearrange("p (t m) -> p t m", t=PACK),
             key_bytes[:].rearrange("p (m t) -> p t m", t=PACK),
         )
         tok_bytes = keep.tile([P, S], U8, name="tok_bytes")
         nc.vector.tensor_copy(tok_bytes[:], x_byte_tab[:].indirect(offs_sb[:]))
-        nc.vector.tensor_copy(plane_words[:, H // 4 :], tok_bytes[:].bitcast(I32))
-        for a in range(1, 4):
-            nc.scalar.dma_start(plane_words[a:P:32, :], plane_words[8 * a : P : 32, :])
-        key_scales = planes[:, :H]
-        tok_scales = planes[:, H:]
+        nc.vector.tensor_copy(scale_rows_i32[:, H // 4 :], tok_bytes[:].bitcast(I32))
+        for a in range(1, QUADRANT // BLOCK_PARTS):
+            nc.scalar.dma_start(scale_rows_i32[a:P:QUADRANT, :], scale_rows_i32[BLOCK_PARTS * a : P : QUADRANT, :])
+        key_scales = scale_rows[:, :H]
+        tok_scales = scale_rows[:, H:]
 
         key_words = keep.tile([P, H], U32, name="key_words")
         nc.vector.tensor_copy(key_words[:], d_word_tab[:].indirect(kidx_sb[:]))
@@ -98,23 +103,23 @@ def tile_picked_simkhopggdiforder_none_p_kernel(
         )
         tok_codes = keep.tile([P, S], U32, name="tok_codes", align_bytes=64)
         for h in range(2):
-            nc.vector.tensor_copy(tok_codes[:, hcols(h)], x_word_tab[:].indirect(half_of(offs_sb, h)))
+            nc.vector.tensor_copy(tok_codes[:, half_cols(h)], x_word_tab[:].indirect(half_list(offs_sb, h)))
 
         s_sb = [win[:, :S] for win in s_win]
         st_sb = [win[:, :S] for win in st_win]
+        s_again = [win[:, S:] for win in st_win]
         sig_at_n1 = keep.tile([P, PACK, S], F32, name="sig_at_n1")
-        s_all = keep.tile([P, PACK, S], F32, name="s_all")
         st_all = keep.tile([P, PACK, S], F32, name="st_all")
         st_at_n2 = keep.tile([P, PACK, S], F32, name="st_at_n2")
         diff = keep.tile([P, PACK, S], F32, name="diff")
         sig_at_n4 = keep.tile([P, PACK, S], F32, name="sig_at_n4")
 
         def scores(t, bank, toks):
-            cols = slice(t * P, (t + 1) * P)
+            keys = slice(t * P, (t + 1) * P)
             nc.tensor.matmul_mx(
                 out=bank,
-                lhsT=key_codes[:, cols].bitcast(FP8X4),
-                lhsT_scale=key_scales[:, cols],
+                lhsT=key_codes[:, keys].bitcast(FP8X4),
+                lhsT_scale=key_scales[:, keys],
                 rhs=tok_codes[:, toks].bitcast(FP8X4),
                 rhs_scale=tok_scales[:, toks],
                 start=True,
@@ -125,15 +130,15 @@ def tile_picked_simkhopggdiforder_none_p_kernel(
             nc.scalar.activation(dst[:, t, :], s_win[t][:].indirect(lst[:]), ACT.Sigmoid)
 
         for h in range(2):
-            bank = psum.tile([P, HALF], F32, name="half_bank%d" % h)
-            scores(0, bank[:], hcols(h))
-            nc.vector.tensor_scalar(s_win[0][:, hcols(h)], bank[:], SIXTEENTH, None, ALU.mult)
-        nc.sync.dma_start(s_all[:, 0, :], s_sb[0])
+            bank = psum.tile([P, HALF], F32, name="s_half_bank%d" % h)
+            scores(0, bank[:], half_cols(h))
+            nc.vector.tensor_scalar(s_win[0][:, half_cols(h)], bank[:], SIXTEENTH, None, ALU.mult)
+        nc.sync.dma_start(s_again[0], s_sb[0])
         for t in range(1, PACK):
             bank = psum.tile([P, S], F32, name="s_bank%d" % t)
             scores(t, bank[:], slice(0, S))
             nc.vector.tensor_scalar(s_sb[t], bank[:], SIXTEENTH, None, ALU.mult)
-            nc.sync.dma_start(s_all[:, t, :], s_sb[t])
+            nc.sync.dma_start(s_again[t], s_sb[t])
         for t in range(PACK):
             sigmoid_at(sig_at_n1, n1_sb, t)
         for t in range(PACK):
@@ -149,26 +154,26 @@ def tile_picked_simkhopggdiforder_none_p_kernel(
             nc.sync.dma_start(st_all[:, t, :], st_sb[t])
             if t > 0:
                 weigh_diff(t - 1)
-            nc.vector.tensor_tensor(diff[:, t, :], s_win[t][:].indirect(n3_sb[:]), s_all[:, t, :], ALU.subtract)
+            nc.vector.tensor_tensor(diff[:, t, :], s_win[t][:].indirect(n3_sb[:]), s_again[t], ALU.subtract)
 
-        last = PACK - 1
         z2_codes = keep.tile([P, S], U32, name="z2_codes", align_bytes=64)
         z2_scales = keep.tile([P, S], U8, name="z2_scales", align_bytes=64)
         z2_bf = [keep.tile([P, PACK * HALF], BF16, name="z2_bf%d" % h, align_bytes=64) for h in range(2)]
 
         def make_z2(h):
             nc.vector.tensor_tensor(
-                z2_bf[h][:].rearrange("p (c i t) -> p c t i", i=2, t=PACK),
-                diff[:, :, hcols(h)].rearrange("p t (c i) -> p c t i", i=2),
-                sig_at_n4[:, :, hcols(h)].rearrange("p t (c i) -> p c t i", i=2),
+                z2_bf[h][:].rearrange("p (c i t) -> p c t i", i=PAIR, t=PACK),
+                diff[:, :, half_cols(h)].rearrange("p t (c i) -> p c t i", i=PAIR),
+                sig_at_n4[:, :, half_cols(h)].rearrange("p t (c i) -> p c t i", i=PAIR),
                 ALU.mult,
             )
 
         def quantise_z2(h):
-            nc.vector.quantize_mx(out=z2_codes[:, hcols(h)].bitcast(FP8X4), scales=z2_scales[:, hcols(h)], in_=z2_bf[h][:])
+            cols = half_cols(h)
+            nc.vector.quantize_mx(out=z2_codes[:, cols].bitcast(FP8X4), scales=z2_scales[:, cols], in_=z2_bf[h][:])
 
         nc.vector.tensor_copy(st_at_n2[:, 0, :], st_win[0][:].indirect(n2_sb[:]))
-        weigh_diff(last)
+        weigh_diff(PACK - 1)
         for t in range(1, PACK):
             nc.scalar.activation(st_at_n2[:, t, :], st_win[t][:].indirect(n2_sb[:]), ACT.Copy)
         make_z2(0)
@@ -178,12 +183,15 @@ def tile_picked_simkhopggdiforder_none_p_kernel(
         z_bf = [keep.tile([P, PACK * P], BF16, name="z_bf%d" % u, align_bytes=64) for u in range(PACK)]
         z_codes = [keep.tile([P, P], U32, name="z_codes%d" % u, align_bytes=64) for u in range(PACK)]
         z_scales = [keep.tile([P, P], U8, name="z_scales%d" % u, align_bytes=64) for u in range(PACK)]
-        st_pairs = st_all[:].rearrange("p t (c u i) -> p u c t i", u=PACK, i=2)
-        n2_pairs = st_at_n2[:].rearrange("p t (c u i) -> p u c t i", u=PACK, i=2)
+        st_pairs = st_all[:].rearrange("p t (c u i) -> p u c t i", u=PACK, i=PAIR)
+        st_at_n2_pairs = st_at_n2[:].rearrange("p t (c u i) -> p u c t i", u=PACK, i=PAIR)
 
         def make_z(u):
             nc.vector.tensor_tensor(
-                z_bf[u][:].rearrange("p (c i t) -> p c t i", i=2, t=PACK), st_pairs[:, u], n2_pairs[:, u], ALU.subtract
+                z_bf[u][:].rearrange("p (c i t) -> p c t i", i=PAIR, t=PACK),
+                st_pairs[:, u],
+                st_at_n2_pairs[:, u],
+                ALU.subtract,
             )
 
         def quantise_z(u):
@@ -198,7 +206,7 @@ def tile_picked_simkhopggdiforder_none_p_kernel(
             quantise_z(u - 1)
         quantise_z(PACK - 1)
 
-        out_rows = out.rearrange("(c u i) n -> u c i n", u=PACK, i=2)
+        out_rows = out.rearrange("(c u i) n -> u c i n", u=PACK, i=PAIR)
         pa = keep.tile([P, PACK, W], F32, name="pa")
         pb = keep.tile([P, PACK, W], F32, name="pb")
         ra = keep.tile([P, PACK, W], F32, name="ra")
@@ -206,7 +214,10 @@ def tile_picked_simkhopggdiforder_none_p_kernel(
         placed = [keep.tile([P, S], F32, name="placed%d" % u) for u in range(PACK)]
         for u in range(PACK):
             cm = keep.tile([P, S], F32, name="cm%d" % u)
-            pieces = [("first", hcols(0)), ("cm", hcols(1))] if u == 0 else [("cm", slice(0, S))]
+            if u == 0:
+                pieces = [("cm_first_half", half_cols(0)), ("cm_shared", half_cols(1))]
+            else:
+                pieces = [("cm_shared", slice(0, S))]
             for tag, cols in pieces:
                 cm_ps = psum.tile([P, cols.stop - cols.start], F32, name="cm_ps", tag=tag)
                 nc.tensor.matmul_mx(
@@ -222,16 +233,16 @@ def tile_picked_simkhopggdiforder_none_p_kernel(
             nc.scalar.activation(pa[:, u, :], cm[:].indirect(n5_sb[:]), ACT.Copy)
             nc.scalar.activation(pb[:, u, :], cm[:].indirect(n6_sb[:]), ACT.Copy)
 
-        def larger(a, b):
-            nc.vector.tensor_tensor(ra[:, a:b, :], pa[:, a:b, :], pb[:, a:b, :], ALU.max)
+        def larger(first, stop):
+            nc.vector.tensor_tensor(ra[:, first:stop, :], pa[:, first:stop, :], pb[:, first:stop, :], ALU.max)
 
-        def smaller(a, b):
-            nc.vector.tensor_tensor(rb[:, a:b, :], pa[:, a:b, :], pb[:, a:b, :], ALU.min)
+        def smaller(first, stop):
+            nc.vector.tensor_tensor(rb[:, first:stop, :], pa[:, first:stop, :], pb[:, first:stop, :], ALU.min)
 
         def put_larger(u):
             nc.vector.tensor_copy(placed[u][:].indirect(n5_sb[:]), ra[:, u, :])
 
-        def put_smaller(u):
+        def put_smaller_and_store(u):
             nc.vector.tensor_copy(placed[u][:].indirect(n6_sb[:]), rb[:, u, :])
             nc.sync.dma_start(out_rows[u], placed[u][:])
 
@@ -240,11 +251,11 @@ def tile_picked_simkhopggdiforder_none_p_kernel(
         larger(1, 2)
         smaller(0, 2)
         put_larger(1)
-        put_smaller(0)
-        put_smaller(1)
+        put_smaller_and_store(0)
+        put_smaller_and_store(1)
         larger(2, 4)
         smaller(2, 4)
         put_larger(2)
         put_larger(3)
-        put_smaller(2)
-        put_smaller(3)
+        put_smaller_and_store(2)
+        put_smaller_and_store(3)

from contextlib import ExitStack

import concourse.mybir as mybir

K, T, S, G, H, W = 512, 2048, 512, 2048, 512, 256
FLOPS = 2 * K * H * S + 2 * H * S * S

F32 = mybir.dt.float32
BF16 = mybir.dt.bfloat16
I32 = mybir.dt.int32
U32 = mybir.dt.uint32
U16 = mybir.dt.uint16
U8 = mybir.dt.uint8
FP8X4 = mybir.dt.float8_e4m3fn_x4
ALU = mybir.AluOpType
ACT = mybir.ActivationFunctionType

P = 128
PACK = 4
GROUP = 16
BLOCK_PARTS = 8
QUADRANT = 32
SCALE_ROWS = K // 32
PAIR = 2
HALF = S // 2
SIXTEENTH = 0.0625


def tile_picked_simkhopggdiforder_none_p_kernel(
    tc, x_words, x_scales, d_words, d_scales, ga, gb, offs, kidx, n1, n2, n3, n4, n5, n6, out
):
    nc = tc.nc
    with ExitStack() as ctx:
        keep = ctx.enter_context(tc.tile_pool(name="keep", bufs=1))
        psum = ctx.enter_context(tc.psum_pool(name="psum", bufs=1))

        def load_list(name, src):
            tile = keep.tile(list(src.shape), U16, name=name)
            nc.sync.dma_start(tile[:], src)
            return tile

        def half_cols(h):
            return slice(h * HALF, (h + 1) * HALF)

        def half_list(lst, h):
            return lst[:, h * (HALF // GROUP) : (h + 1) * (HALF // GROUP)]

        d_word_tab = keep.tile([P, G], U32, name="d_word_tab")
        x_word_tab = keep.tile([P, T], U32, name="x_word_tab")
        d_byte_tab = keep.tile([P, G], U8, name="d_byte_tab")
        x_byte_tab = keep.tile([P, T], U8, name="x_byte_tab")

        def load_scale_rows(tab, scales):
            rows = scales[0].bitcast(I32)
            nc.sync.dma_start(
                tab[:].bitcast(I32), rows.unsqueeze(1).broadcast_to([SCALE_ROWS, BLOCK_PARTS, rows.shape[1]])
            )

        load_scale_rows(d_byte_tab, d_scales)
        kidx_sb = load_list("kidx_sb", kidx)
        offs_sb = load_list("offs_sb", offs)
        load_scale_rows(x_byte_tab, x_scales)
        n1_sb = load_list("n1_sb", n1)
        n3_sb = load_list("n3_sb", n3)
        nc.sync.dma_start(d_word_tab[:].bitcast(I32), d_words[0].rearrange("p n r -> p (n r)").bitcast(I32))
        nc.sync.dma_start(x_word_tab[:].bitcast(I32), x_words[0].rearrange("p n r -> p (n r)").bitcast(I32))
        n4_sb = load_list("n4_sb", n4)
        n2_sb = load_list("n2_sb", n2)
        n5_sb = load_list("n5_sb", n5)
        n6_sb = load_list("n6_sb", n6)

        s_win = [keep.tile([P, 2 * S], F32, name="s_win%d" % t) for t in range(PACK)]
        st_win = [keep.tile([P, 2 * S], F32, name="st_win%d" % t) for t in range(PACK)]
        for t in range(PACK):
            nc.vector.memset(s_win[t][:, S:], 0.0)
        ga_sb = keep.tile([P, PACK], F32, name="ga_sb")
        gb_sb = keep.tile([P, PACK], F32, name="gb_sb")
        nc.gpsimd.dma_start(ga_sb[:], ga.rearrange("(p t) o -> p (t o)", t=PACK))
        nc.gpsimd.dma_start(gb_sb[:], gb.rearrange("(p t) o -> p (t o)", t=PACK))

        key_bytes = keep.tile([P, H], U8, name="key_bytes")
        nc.vector.tensor_copy(key_bytes[:], d_byte_tab[:].indirect(kidx_sb[:]))
        scale_rows = keep.tile([P, H + S], U8, name="scale_rows", align_bytes=64)
        scale_rows_i32 = scale_rows[:].bitcast(I32)
        nc.vector.tensor_copy(
            scale_rows[:, :H].rearrange("p (t m) -> p t m", t=PACK),
            key_bytes[:].rearrange("p (m t) -> p t m", t=PACK),
        )
        tok_bytes = keep.tile([P, S], U8, name="tok_bytes")
        nc.vector.tensor_copy(tok_bytes[:], x_byte_tab[:].indirect(offs_sb[:]))
        nc.vector.tensor_copy(scale_rows_i32[:, H // 4 :], tok_bytes[:].bitcast(I32))
        for a in range(1, QUADRANT // BLOCK_PARTS):
            nc.scalar.dma_start(scale_rows_i32[a:P:QUADRANT, :], scale_rows_i32[BLOCK_PARTS * a : P : QUADRANT, :])
        key_scales = scale_rows[:, :H]
        tok_scales = scale_rows[:, H:]

        key_words = keep.tile([P, H], U32, name="key_words")
        nc.vector.tensor_copy(key_words[:], d_word_tab[:].indirect(kidx_sb[:]))
        key_codes = keep.tile([P, H], U32, name="key_codes", align_bytes=64)
        nc.vector.tensor_copy(
            key_codes[:].rearrange("p (t m) -> p m t", t=PACK),
            key_words[:].rearrange("p (m t) -> p m t", t=PACK),
        )
        tok_codes = keep.tile([P, S], U32, name="tok_codes", align_bytes=64)
        for h in range(2):
            nc.vector.tensor_copy(tok_codes[:, half_cols(h)], x_word_tab[:].indirect(half_list(offs_sb, h)))

        s_sb = [win[:, :S] for win in s_win]
        st_sb = [win[:, :S] for win in st_win]
        s_again = [win[:, S:] for win in st_win]
        sig_at_n1 = keep.tile([P, PACK, S], F32, name="sig_at_n1")
        st_all = keep.tile([P, PACK, S], F32, name="st_all")
        st_at_n2 = keep.tile([P, PACK, S], F32, name="st_at_n2")
        diff = keep.tile([P, PACK, S], F32, name="diff")
        sig_at_n4 = keep.tile([P, PACK, S], F32, name="sig_at_n4")

        def scores(t, bank, toks):
            keys = slice(t * P, (t + 1) * P)
            nc.tensor.matmul_mx(
                out=bank,
                lhsT=key_codes[:, keys].bitcast(FP8X4),
                lhsT_scale=key_scales[:, keys],
                rhs=tok_codes[:, toks].bitcast(FP8X4),
                rhs_scale=tok_scales[:, toks],
                start=True,
                stop=True,
            )

        def sigmoid_at(dst, lst, t):
            nc.scalar.activation(dst[:, t, :], s_win[t][:].indirect(lst[:]), ACT.Sigmoid)

        for h in range(2):
            bank = psum.tile([P, HALF], F32, name="s_half_bank%d" % h)
            scores(0, bank[:], half_cols(h))
            nc.vector.tensor_scalar(s_win[0][:, half_cols(h)], bank[:], SIXTEENTH, None, ALU.mult)
        nc.sync.dma_start(s_again[0], s_sb[0])
        for t in range(1, PACK):
            bank = psum.tile([P, S], F32, name="s_bank%d" % t)
            scores(t, bank[:], slice(0, S))
            nc.vector.tensor_scalar(s_sb[t], bank[:], SIXTEENTH, None, ALU.mult)
            nc.sync.dma_start(s_again[t], s_sb[t])
        for t in range(PACK):
            sigmoid_at(sig_at_n1, n1_sb, t)
        for t in range(PACK):
            sigmoid_at(sig_at_n4, n4_sb, t)

        def weigh_diff(t):
            nc.vector.tensor_scalar(diff[:, t, :], diff[:, t, :], gb_sb[:, t : t + 1], -1.0, ALU.mult, ALU.mult)

        for t in range(PACK):
            nc.vector.scalar_tensor_tensor(
                st_sb[t], s_sb[t], ga_sb[:, t : t + 1], sig_at_n1[:, t, :], ALU.mult, ALU.mult
            )
            nc.sync.dma_start(st_all[:, t, :], st_sb[t])
            if t > 0:
                weigh_diff(t - 1)
            nc.vector.tensor_tensor(diff[:, t, :], s_win[t][:].indirect(n3_sb[:]), s_again[t], ALU.subtract)

        z2_codes = keep.tile([P, S], U32, name="z2_codes", align_bytes=64)
        z2_scales = keep.tile([P, S], U8, name="z2_scales", align_bytes=64)
        z2_bf = [keep.tile([P, PACK * HALF], BF16, name="z2_bf%d" % h, align_bytes=64) for h in range(2)]

        def make_z2(h):
            nc.vector.tensor_tensor(
                z2_bf[h][:].rearrange("p (c i t) -> p c t i", i=PAIR, t=PACK),
                diff[:, :, half_cols(h)].rearrange("p t (c i) -> p c t i", i=PAIR),
                sig_at_n4[:, :, half_cols(h)].rearrange("p t (c i) -> p c t i", i=PAIR),
                ALU.mult,
            )

        def quantise_z2(h):
            cols = half_cols(h)
            nc.vector.quantize_mx(out=z2_codes[:, cols].bitcast(FP8X4), scales=z2_scales[:, cols], in_=z2_bf[h][:])

        nc.vector.tensor_copy(st_at_n2[:, 0, :], st_win[0][:].indirect(n2_sb[:]))
        weigh_diff(PACK - 1)
        for t in range(1, PACK):
            nc.scalar.activation(st_at_n2[:, t, :], st_win[t][:].indirect(n2_sb[:]), ACT.Copy)
        make_z2(0)
        make_z2(1)
        quantise_z2(0)

        z_bf = [keep.tile([P, PACK * P], BF16, name="z_bf%d" % u, align_bytes=64) for u in range(PACK)]
        z_codes = [keep.tile([P, P], U32, name="z_codes%d" % u, align_bytes=64) for u in range(PACK)]
        z_scales = [keep.tile([P, P], U8, name="z_scales%d" % u, align_bytes=64) for u in range(PACK)]
        st_pairs = st_all[:].rearrange("p t (c u i) -> p u c t i", u=PACK, i=PAIR)
        st_at_n2_pairs = st_at_n2[:].rearrange("p t (c u i) -> p u c t i", u=PACK, i=PAIR)

        def make_z(u):
            nc.vector.tensor_tensor(
                z_bf[u][:].rearrange("p (c i t) -> p c t i", i=PAIR, t=PACK),
                st_pairs[:, u],
                st_at_n2_pairs[:, u],
                ALU.subtract,
            )

        def quantise_z(u):
            nc.vector.quantize_mx(out=z_codes[u][:].bitcast(FP8X4), scales=z_scales[u][:], in_=z_bf[u][:])

        make_z(0)
        quantise_z2(1)
        quantise_z(0)
        make_z(1)
        for u in range(2, PACK):
            make_z(u)
            quantise_z(u - 1)
        quantise_z(PACK - 1)

        out_rows = out.rearrange("(c u i) n -> u c i n", u=PACK, i=PAIR)
        pa = keep.tile([P, PACK, W], F32, name="pa")
        pb = keep.tile([P, PACK, W], F32, name="pb")
        ra = keep.tile([P, PACK, W], F32, name="ra")
        rb = keep.tile([P, PACK, W], F32, name="rb")
        placed = [keep.tile([P, S], F32, name="placed%d" % u) for u in range(PACK)]
        for u in range(PACK):
            cm = keep.tile([P, S], F32, name="cm%d" % u)
            if u == 0:
                pieces = [("cm_first_half", half_cols(0)), ("cm_shared", half_cols(1))]
            else:
                pieces = [("cm_shared", slice(0, S))]
            for tag, cols in pieces:
                cm_ps = psum.tile([P, cols.stop - cols.start], F32, name="cm_ps", tag=tag)
                nc.tensor.matmul_mx(
                    out=cm_ps[:],
                    lhsT=z_codes[u][:].bitcast(FP8X4),
                    lhsT_scale=z_scales[u][:],
                    rhs=z2_codes[:, cols].bitcast(FP8X4),
                    rhs_scale=z2_scales[:, cols],
                    start=True,
                    stop=True,
                )
                nc.scalar.activation(cm[:, cols], cm_ps[:], ACT.Copy, scale=SIXTEENTH)
            nc.scalar.activation(pa[:, u, :], cm[:].indirect(n5_sb[:]), ACT.Copy)
            nc.scalar.activation(pb[:, u, :], cm[:].indirect(n6_sb[:]), ACT.Copy)

        def larger(first, stop):
            nc.vector.tensor_tensor(ra[:, first:stop, :], pa[:, first:stop, :], pb[:, first:stop, :], ALU.max)

        def smaller(first, stop):
            nc.vector.tensor_tensor(rb[:, first:stop, :], pa[:, first:stop, :], pb[:, first:stop, :], ALU.min)

        def put_larger(u):
            nc.vector.tensor_copy(placed[u][:].indirect(n5_sb[:]), ra[:, u, :])

        def put_smaller_and_store(u):
            nc.vector.tensor_copy(placed[u][:].indirect(n6_sb[:]), rb[:, u, :])
            nc.sync.dma_start(out_rows[u], placed[u][:])

        larger(0, 1)
        put_larger(0)
        larger(1, 2)
        smaller(0, 2)
        put_larger(1)
        put_smaller_and_store(0)
        put_smaller_and_store(1)
        larger(2, 4)
        smaller(2, 4)
        put_larger(2)
        put_larger(3)
        put_smaller_and_store(2)
        put_smaller_and_store(3)
